import numpy as np
import ml_dtypes


def mxq(x, axis, fmt="e4m3"):
    dtype, down = {"e4m3": (ml_dtypes.float8_e4m3fn, 7), "e5m2": (ml_dtypes.float8_e5m2, 14)}[fmt]
    v = np.moveaxis(np.asarray(x, np.float32).astype(ml_dtypes.bfloat16).astype(np.float64), axis, -1)
    blocks = v.reshape(v.shape[:-1] + (-1, 32))
    amax = np.abs(blocks).max(-1, keepdims=True)
    byte = np.maximum(np.where(amax > 0, np.frexp(amax)[1] - 1 + 127, 0) - down, 1)
    scale = np.exp2(byte - 127.0)
    codes = (blocks / scale).astype(np.float32).astype(dtype).astype(np.float64)
    return np.moveaxis((codes * scale).reshape(v.shape), -1, axis)


WIDE = False


def mx_kscale(k):
    if not WIDE:
        return np.ones(k)
    levels = np.array([10, -10, 5, -5, 0])
    if k % 512:
        return np.exp2(np.random.permutation(np.resize(levels, k // 32))).repeat(32)
    a = np.empty((k // 512, 16))
    for p in range(k // 512):
        a[p, :8] = np.random.permutation(np.resize(levels, 8))
        for g in range(8):
            far = levels[np.abs(levels - a[p, g]) >= 10]
            a[p, g + 8] = far[np.random.randint(len(far))]
    return np.exp2(a.ravel()).repeat(32)


def f64(x):
    return np.asarray(x).astype(np.float64)


def striped(idx):
    return np.tile(idx.reshape(-1, 16).T, (8, 1)).astype(np.uint16)


def unstriped(offs):
    return offs[:16].T.reshape(-1).astype(np.int64)


def striped8(idx):
    return np.concatenate([x.reshape(-1, 16).T for x in idx]).astype(np.uint16)


def runs(offs, k):
    lists = np.stack([offs[16 * r : 16 * r + 16].T.reshape(-1) for r in range(8)]).astype(np.int64)
    return lists[np.arange(k) % 512 // 64]


def pack_weight(w):
    k, n = w.shape
    w = f64(np.asarray(w, np.float32).astype(ml_dtypes.bfloat16)).reshape(k // 32, 32, n)
    amax = np.abs(w).max(1)
    byte = np.clip(np.where(amax > 0, np.frexp(amax)[1] - 1 + 127 - 7, 1), 1, 254)
    scaled = (w * np.exp2(127.0 - byte)[:, None, :]).reshape(k, n).astype(np.float32)
    words = np.ascontiguousarray(scaled.reshape(k // 512, 128, 4, n).transpose(0, 1, 3, 2)).astype(ml_dtypes.float8_e4m3fn).view(np.uint8)
    return words, np.ascontiguousarray(byte.astype(np.uint8).reshape(k // 512, 16, n))


def unpack_weight(words, scales):
    g, p, n, _ = words.shape
    vals = np.ascontiguousarray(words).view(ml_dtypes.float8_e4m3fn).astype(np.float64) * np.repeat(np.exp2(scales.astype(np.float64) - 127.0), 8, axis=1)[..., None]
    return vals.transpose(0, 1, 3, 2).reshape(g * 512, n)


E2M1 = np.array([0.0, 0.5, 1.0, 1.5, 2.0, 3.0, 4.0, 6.0, -0.0, -0.5, -1.0, -1.5, -2.0, -3.0, -4.0, -6.0])


def pack_fp4(w):
    k, n = w.shape
    w = f64(np.asarray(w, np.float32).astype(ml_dtypes.bfloat16)).reshape(k // 32, 32, n)
    amax = np.abs(w).max(1)
    mant, ex = np.frexp(amax / 6.0)
    byte = np.clip(np.where(amax > 0, np.where(mant > 0.5, ex, ex - 1) + 127, 1), 1, 254)
    scaled = (w * np.exp2(127.0 - byte)[:, None, :]).reshape(k, n).astype(np.float32)
    c = np.ascontiguousarray(scaled.reshape(k // 512, 128, 4, n).transpose(0, 1, 3, 2)).astype(ml_dtypes.float4_e2m1fn).view(np.uint8) & 0xF
    words = (c[..., 0::2] | (c[..., 1::2] << 4)).reshape(k // 512, 128, 2 * n)
    return np.ascontiguousarray(words), np.ascontiguousarray(byte.astype(np.uint8).reshape(k // 512, 16, n))


def unpack_fp4(words, scales):
    g, _, n = scales.shape
    words = np.ascontiguousarray(words).reshape(g, 128, n, 2)
    nib = np.empty((g, 128, n, 4), np.uint8)
    nib[..., 0::2] = words & 0xF
    nib[..., 1::2] = words >> 4
    vals = E2M1[nib] * np.repeat(np.exp2(scales.astype(np.float64) - 127.0), 8, axis=1)[..., None]
    return vals.transpose(0, 1, 3, 2).reshape(g * 512, n)


def planes(y):
    n, m = y.shape
    v = y.astype(np.float32).astype(ml_dtypes.bfloat16).astype(np.float64).reshape(n // 32, 32, m)
    top = np.abs(v).max(1)
    byte = np.clip(np.where(top > 0, np.frexp(top)[1] - 1 + 127 - 7, 1), 1, 254)
    codes = (v * np.exp2(127.0 - byte)[:, None, :]).reshape(n, m).astype(np.float32).astype(ml_dtypes.float8_e4m3fn).view(np.uint8)
    words = codes.reshape(n // 512, 128, 4, m).transpose(0, 1, 3, 2)
    return np.ascontiguousarray(words), np.ascontiguousarray(byte.astype(np.uint8).reshape(n // 512, 16, m))


K, T, S, H, W, C = 512, 2048, 512, 512, 256, 512


def setup_inputs():
    n = np.random.standard_normal
    s = mx_kscale(K)[:, None]
    packed_xT = pack_weight(n((K, T)) * s)
    packed_w1 = pack_fp4(n((K, H)) / np.sqrt(K) / s)
    perm = np.random.permutation(S)
    return {
        "x_words": packed_xT[0],
        "x_scales": packed_xT[1],
        "w1_words": packed_w1[0],
        "w1_scales": packed_w1[1],
        "gs": (np.random.uniform(0.5, 1.5, (K, 1)) / s).astype(np.float32),
        "offs": striped(np.random.permutation(T)[:S]),
        "n1": striped(perm[:W]),
        "n2": striped(perm[W:]),
        "ca": striped(np.random.permutation(T)[:C]),
        "hc": striped8(np.random.randint(0, T, (8, C))),
        "n3": striped(np.random.permutation(S)),
        "n4": striped(np.random.permutation(S)),
        "n5": striped(np.random.permutation(S)),
        "n6": striped(np.random.permutation(S)),
    }


def reference(x_words, x_scales, w1_words, w1_scales, gs, offs, n1, n2, ca, hc, n3, n4, n5, n6):
    x_ca = unpack_weight(x_words, x_scales)[:, unstriped(ca)]
    xq = unpack_weight(x_words, x_scales)[:, unstriped(offs)]
    y = unpack_fp4(w1_words, w1_scales).T @ xq
    pa = y[:, unstriped(n1)]
    pb = y[:, unstriped(n2)]
    rb = np.minimum(pa, pb)
    ra = np.maximum(pa, pb)
    ds = np.zeros((H, S))
    ds[:, unstriped(n1)] = ra
    dt = ds.copy()
    dt[:, unstriped(n2)] = rb
    z = f64(gs) * dt
    zq = mxq(z, 0, "e4m3")
    a = 0.0625 * (x_ca.T @ zq)
    x_hc = unpack_weight(x_words, x_scales)[np.arange(K)[:, None], runs(hc, K)]
    b = 0.0625 * (x_hc.T @ zq)
    out_0 = np.maximum(a[:, unstriped(n3)] + b[:, unstriped(n5)], a[:, unstriped(n4)] + b[:, unstriped(n6)])
    return (out_0,) + planes(out_0)

@@ -1,0 +1,222 @@
+from contextlib import ExitStack
+
+import concourse.mybir as mybir
+
+K, T, S, H, W, C = 512, 2048, 512, 512, 256, 512
+FLOPS = 2 * K * H * S + 2 * 2 * K * C * S
+
+F32 = mybir.dt.float32
+BF16 = mybir.dt.bfloat16
+I32 = mybir.dt.int32
+U32 = mybir.dt.uint32
+U16 = mybir.dt.uint16
+U8 = mybir.dt.uint8
+FP8X4 = mybir.dt.float8_e4m3fn_x4
+FP4X4 = mybir.dt.float4_e2m1fn_x4
+ALU = mybir.AluOpType
+COPY = mybir.ActivationFunctionType.Copy
+
+P = 128
+PACK = 4
+SPARE = 16
+SCORE_SCALE = 0.0625
+
+
+def tile_picked_cdhpathborder_none_po_kernel(
+    tc, x_words, x_scales, w1_words, w1_scales, gs, offs, n1, n2, ca, hc, n3, n4, n5, n6, out_0, out_1, out_2
+):
+    nc = tc.nc
+    with ExitStack() as ctx:
+        lists = ctx.enter_context(tc.tile_pool(name="lists", bufs=1))
+        sb = ctx.enter_context(tc.tile_pool(name="sb", bufs=1))
+        psum = ctx.enter_context(tc.psum_pool(name="psum", bufs=8))
+
+        def load_list(name, dram):
+            tile = lists.tile(list(dram.shape), U16, name=name)
+            nc.sync.dma_start(tile[:], dram)
+            return tile
+
+        def new(name, shape, dtype, tag=None):
+            return sb.tile(shape, dtype, name=name, tag=tag or name, align_bytes=64)
+
+        xs_rows = x_scales[0].bitcast(I32)
+        w1s_rows = w1_scales[0].bitcast(I32)
+
+        xs = new("xs", [P, T], U8)
+        w1s = new("w1s", [P, H], U8)
+        xs_runs = new("xs_runs", [P, T], U8)
+        hc_plane = new("hc_plane", [P, C], U8)
+        nc.gpsimd.memset(xs[:].bitcast(I32), 0)
+        nc.vector.memset(w1s[:].bitcast(I32), 0)
+        nc.gpsimd.memset(xs_runs[:].bitcast(I32), 0)
+        nc.gpsimd.memset(hc_plane[:].bitcast(I32), 0)
+        a_sb = [new("a%d" % t, [P, S + SPARE], F32) for t in range(PACK)]
+        b_sb = [new("b%d" % t, [P, S + SPARE], F32) for t in range(PACK)]
+        for tile in a_sb + b_sb:
+            nc.gpsimd.memset(tile[:, S:], 0.0)
+
+        offs_t = load_list("offs_t", offs)
+        w1w = new("w1w", [P, 2 * H], U8)
+        nc.sync.dma_start(w1w[:].bitcast(I32), w1_words[0].bitcast(I32))
+        for q in range(4):
+            nc.sync.dma_start(xs[32 * q : 32 * q + 4, :].bitcast(I32), xs_rows[4 * q : 4 * q + 4, :])
+        xw = new("xw", [P, T], U32)
+        nc.sync.dma_start(xw[:].bitcast(I32), x_words[0].rearrange("p n t -> p (n t)").bitcast(I32))
+        for q in range(4):
+            nc.sync.dma_start(w1s[32 * q : 32 * q + 4, :].bitcast(I32), w1s_rows[4 * q : 4 * q + 4, :])
+        ca_t = load_list("ca_t", ca)
+        n1_t = load_list("n1_t", n1)
+        n2_t = load_list("n2_t", n2)
+        hc_t = load_list("hc_t", hc)
+        for e in range(2):
+            nc.sync.dma_start(xs_runs[e:P:16, :].bitcast(I32), xs_rows[e:16:2, :])
+        gs_t = new("gs_t", [P, PACK], F32)
+        nc.sync.dma_start(gs_t[:], gs.rearrange("(p t) o -> p (t o)", t=PACK))
+        n3_t = load_list("n3_t", n3)
+        n4_t = load_list("n4_t", n4)
+        n5_t = load_list("n5_t", n5)
+        n6_t = load_list("n6_t", n6)
+
+        def deal(name, src, dtype):
+            dealt = new(name, [P, C], dtype)
+            nc.vector.tensor_copy(
+                dealt[:].rearrange("p (t m) -> p t m", t=PACK), src[:].rearrange("p (m t) -> p t m", t=PACK)
+            )
+            return dealt
+
+        def pick(name, table, offsets, dtype, tag=None):
+            picked = new(name, [P, C], dtype, tag)
+            nc.vector.tensor_copy(picked[:], table[:].indirect(offsets[:]))
+            return picked
+
+        w1w_d = new("w1w_d", [P, 2 * H], U8)
+        nc.vector.tensor_copy(
+            w1w_d[:].rearrange("p (t m b) -> p t m b", t=PACK, b=2), w1w[:].rearrange("p (m t b) -> p t m b", t=PACK, b=2)
+        )
+        xq_s = pick("xq_s", xs, offs_t, U8)
+        xq_w = pick("xq_w", xw, offs_t, U32)
+        w1s_d = deal("w1s_d", w1s, U8)
+
+        y_ps = []
+        for t in range(PACK):
+            bank = psum.tile([P, S], F32, name="bank", tag="bank")
+            nc.tensor.matmul_mx(
+                out=bank[:],
+                lhsT=w1w_d[:, 2 * P * t : 2 * P * (t + 1)].bitcast(FP4X4),
+                lhsT_scale=w1s_d[:, P * t : P * (t + 1)],
+                rhs=xq_w[:].bitcast(FP8X4),
+                rhs_scale=xq_s[:],
+                start=True,
+                stop=True,
+            )
+            y_ps.append(bank)
+
+        ca_s = deal("ca_s_d", pick("ca_s", xs, ca_t, U8), U8)
+        ca_w = new("ca_w", [P, C], U32)
+        nc.vector.tensor_copy(ca_w[:].rearrange("p (t m) -> p m t", t=PACK), xw[:].indirect(ca_t[:]))
+        hc_s = deal("hc_s_d", pick("hc_s", xs_runs, hc_t, U8), U8)
+        for r in range(4):
+            src = 16 * (r // 2) + r % 2
+            nc.sync.dma_start(hc_plane[r:P:32, :].bitcast(I32), hc_s[src:P:32, :].bitcast(I32))
+
+        pa, pb, ra, rb, dt = [], [], [], [], []
+        for t in range(PACK):
+            y = new("y%d" % t, [P, S], F32)
+            nc.scalar.copy(y[:], y_ps[t][:])
+            pa.append(new("pa%d" % t, [P, W], F32))
+            pb.append(new("pb%d" % t, [P, W], F32))
+            nc.scalar.activation(pa[t][:], y[:].indirect(n1_t[:]), COPY)
+            nc.scalar.activation(pb[t][:], y[:].indirect(n2_t[:]), COPY)
+            ra.append(new("ra%d" % t, [P, W], F32))
+            rb.append(new("rb%d" % t, [P, W], F32))
+            dt.append(new("dt%d" % t, [P, S], F32))
+
+        zp = new("zp", [P, 2, S, 2], BF16)
+
+        def order(t):
+            nc.vector.tensor_tensor(ra[t][:], pa[t][:], pb[t][:], ALU.max)
+            nc.vector.tensor_tensor(rb[t][:], pa[t][:], pb[t][:], ALU.min)
+
+        def put_vector(t):
+            nc.vector.tensor_copy(dt[t][:].indirect(n1_t[:]), ra[t][:])
+            nc.vector.tensor_copy(dt[t][:].indirect(n2_t[:]), rb[t][:])
+
+        def put_scalar(t):
+            nc.scalar.activation(dt[t][:].indirect(n1_t[:]), ra[t][:], COPY)
+            nc.scalar.activation(dt[t][:].indirect(n2_t[:]), rb[t][:], COPY)
+
+        def weigh(t):
+            nc.vector.tensor_scalar(zp[:, t // 2, :, t % 2], dt[t][:], gs_t[:, t : t + 1], None, ALU.mult)
+
+        order(0)
+        order(1)
+        put_scalar(0)
+        put_scalar(1)
+        order(2)
+        put_vector(2)
+        order(3)
+        put_vector(3)
+        for t in (2, 3, 0, 1):
+            weigh(t)
+        z4 = new("z4", [P, S * PACK], BF16)
+        nc.vector.tensor_copy(
+            z4[:].bitcast(F32).rearrange("p (j u) -> p j u", u=2),
+            zp[:].rearrange("p u j e -> p u (j e)").bitcast(F32).rearrange("p u j -> p j u"),
+        )
+        z_w = new("z_w", [P, S], U32)
+        z_s = new("z_s", [P, S], U8)
+        nc.vector.quantize_mx(out=z_w[:].bitcast(FP8X4), scales=z_s[:], in_=z4[:])
+        hc_w = deal("hc_w_d", pick("hc_w", xw, hc_t, U32, tag="z4"), U32)
+
+        def score(words, plane, t):
+            bank = psum.tile([P, S], F32, name="bank", tag="bank")
+            nc.tensor.matmul_mx(
+                out=bank[:],
+                lhsT=words[:, P * t : P * (t + 1)].bitcast(FP8X4),
+                lhsT_scale=plane[:, P * t : P * (t + 1)],
+                rhs=z_w[:].bitcast(FP8X4),
+                rhs_scale=z_s[:],
+                start=True,
+                stop=True,
+            )
+            return bank
+
+        res = new("res", [P, PACK, S], F32)
+        out_rows = out_0.rearrange("(p t) j -> p t j", t=PACK)
+        res4 = new("res4", [P, S * PACK], BF16)
+        res_w = new("res_w", [P, S], U32)
+        res_s = new("res_s", [P, S], U8)
+        out_words = out_1[0].rearrange("p n t -> p (n t)").bitcast(I32)
+        out_scales = out_2[0].bitcast(I32)
+        for t in range(PACK):
+            a_ps = score(ca_w, ca_s, t)
+            b_ps = score(hc_w, hc_plane, t)
+            nc.scalar.activation(a_sb[t][:, :S], a_ps[:], COPY, scale=SCORE_SCALE)
+            if t < 1:
+                nc.vector.tensor_scalar(b_sb[t][:, :S], b_ps[:], SCORE_SCALE, None, ALU.mult)
+            else:
+                nc.scalar.activation(b_sb[t][:, :S], b_ps[:], COPY, scale=SCORE_SCALE)
+            a3 = new("a3_%d" % t, [P, S], F32)
+            a4 = new("a4_%d" % t, [P, S], F32)
+            s1 = new("s1_%d" % t, [P, S], F32)
+            s2 = new("s2_%d" % t, [P, S], F32)
+            pieces = [(0, S)] if t < PACK - 1 else [(0, S // 2), (S // 2, S)]
+            for lo, hi in pieces:
+                cols = slice(lo // 16, hi // 16)
+                nc.scalar.activation(a3[:, lo:hi], a_sb[t][:].indirect(n3_t[:, cols]), COPY)
+                nc.scalar.activation(a4[:, lo:hi], a_sb[t][:].indirect(n4_t[:, cols]), COPY)
+                nc.vector.tensor_tensor(s1[:, lo:hi], b_sb[t][:].indirect(n5_t[:, cols]), a3[:, lo:hi], ALU.add)
+                nc.vector.tensor_tensor(s2[:, lo:hi], b_sb[t][:].indirect(n6_t[:, cols]), a4[:, lo:hi], ALU.add)
+                nc.vector.tensor_tensor(res[:, t, lo:hi], s1[:, lo:hi], s2[:, lo:hi], ALU.max)
+                nc.sync.dma_start(out_rows[:, t, lo:hi], res[:, t, lo:hi])
+                if t == PACK - 1:
+                    (nc.scalar.copy if lo == 0 else nc.vector.tensor_copy)(
+                        res4[:, PACK * lo : PACK * hi].rearrange("p (c i t) -> p c t i", i=4, t=PACK),
+                        res[:, :, lo:hi].rearrange("p t (c i) -> p c t i", i=4),
+                    )
+                    nc.vector.quantize_mx(
+                        out=res_w[:, lo:hi].bitcast(FP8X4), scales=res_s[:, lo:hi], in_=res4[:, PACK * lo : PACK * hi]
+                    )
+                    nc.sync.dma_start(out_words[:, lo:hi], res_w[:, lo:hi].bitcast(I32))
+        for q in range(4):
+            nc.scalar.dma_start(out_scales[4 * q : 4 * q + 4, :], res_s[32 * q : 32 * q + 4, :].bitcast(I32))

@@ -20,6 +20,7 @@ P = 128
 PACK = 4
 SPARE = 16
 SCORE_SCALE = 0.0625
+HALF = S // 2
 
 
 def tile_picked_cdhpathborder_none_po_kernel(
@@ -111,112 +112,140 @@ def tile_picked_cdhpathborder_none_po_kernel(
             )
             y_ps.append(bank)
 
-        ca_s = deal("ca_s_d", pick("ca_s", xs, ca_t, U8), U8)
+        cand_s = new("cand_s", [P, 2, C], U8)
+        nc.vector.tensor_copy(cand_s[:, 0, :], xs[:].indirect(ca_t[:]))
+        nc.vector.tensor_copy(cand_s[:, 1, :], xs_runs[:].indirect(hc_t[:]))
         ca_w = new("ca_w", [P, C], U32)
         nc.vector.tensor_copy(ca_w[:].rearrange("p (t m) -> p m t", t=PACK), xw[:].indirect(ca_t[:]))
-        hc_s = deal("hc_s_d", pick("hc_s", xs_runs, hc_t, U8), U8)
+        cand_s_d = new("cand_s_d", [P, 2, C], U8)
+        nc.vector.tensor_copy(
+            cand_s_d[:].rearrange("p l (t m) -> p l t m", t=PACK), cand_s[:].rearrange("p l (m t) -> p l t m", t=PACK)
+        )
+        ca_s = cand_s_d[:, 0, :]
         for r in range(4):
             src = 16 * (r // 2) + r % 2
-            nc.sync.dma_start(hc_plane[r:P:32, :].bitcast(I32), hc_s[src:P:32, :].bitcast(I32))
+            nc.sync.dma_start(hc_plane[r:P:32, :].bitcast(I32), cand_s_d[src:P:32, 1, :].bitcast(I32))
 
-        pa, pb, ra, rb, dt = [], [], [], [], []
+        y = [new("y%d" % t, [P, S], F32) for t in range(PACK)]
+        pa = [new("pa%d" % t, [P, W], F32) for t in range(PACK)]
+        pb = [new("pb%d" % t, [P, W], F32) for t in range(PACK)]
+        ra = [new("ra%d" % t, [P, W], F32) for t in range(PACK)]
+        rb = [new("rb%d" % t, [P, W], F32) for t in range(PACK)]
+        dt = [new("dt%d" % t, [P, S], F32) for t in range(PACK)]
+        nc.scalar.copy(y[0][:], y_ps[0][:])
         for t in range(PACK):
-            y = new("y%d" % t, [P, S], F32)
-            nc.scalar.copy(y[:], y_ps[t][:])
-            pa.append(new("pa%d" % t, [P, W], F32))
-            pb.append(new("pb%d" % t, [P, W], F32))
-            nc.scalar.activation(pa[t][:], y[:].indirect(n1_t[:]), COPY)
-            nc.scalar.activation(pb[t][:], y[:].indirect(n2_t[:]), COPY)
-            ra.append(new("ra%d" % t, [P, W], F32))
-            rb.append(new("rb%d" % t, [P, W], F32))
-            dt.append(new("dt%d" % t, [P, S], F32))
-
-        zp = new("zp", [P, 2, S, 2], BF16)
-
-        def order(t):
+            if t + 1 < PACK:
+                nc.scalar.copy(y[t + 1][:], y_ps[t + 1][:])
+            nc.scalar.activation(pa[t][:], y[t][:].indirect(n1_t[:]), COPY)
+            nc.scalar.activation(pb[t][:], y[t][:].indirect(n2_t[:]), COPY)
+        for t in range(PACK):
             nc.vector.tensor_tensor(ra[t][:], pa[t][:], pb[t][:], ALU.max)
             nc.vector.tensor_tensor(rb[t][:], pa[t][:], pb[t][:], ALU.min)
-
-        def put_vector(t):
             nc.vector.tensor_copy(dt[t][:].indirect(n1_t[:]), ra[t][:])
-            nc.vector.tensor_copy(dt[t][:].indirect(n2_t[:]), rb[t][:])
-
-        def put_scalar(t):
-            nc.scalar.activation(dt[t][:].indirect(n1_t[:]), ra[t][:], COPY)
+        for t in range(PACK):
             nc.scalar.activation(dt[t][:].indirect(n2_t[:]), rb[t][:], COPY)
 
-        def weigh(t):
-            nc.vector.tensor_scalar(zp[:, t // 2, :, t % 2], dt[t][:], gs_t[:, t : t + 1], None, ALU.mult)
-
-        order(0)
-        order(1)
-        put_scalar(0)
-        put_scalar(1)
-        order(2)
-        put_vector(2)
-        order(3)
-        put_vector(3)
-        for t in (2, 3, 0, 1):
-            weigh(t)
-        z4 = new("z4", [P, S * PACK], BF16)
-        nc.vector.tensor_copy(
-            z4[:].bitcast(F32).rearrange("p (j u) -> p j u", u=2),
-            zp[:].rearrange("p u j e -> p u (j e)").bitcast(F32).rearrange("p u j -> p j u"),
-        )
+        halves = [slice(0, HALF), slice(HALF, S)]
+        zp = [new("zp%d" % h, [P, 2, HALF, 2], BF16) for h in range(2)]
+        for t in range(PACK):
+            for h in range(2):
+                nc.vector.tensor_scalar(zp[h][:, t // 2, :, t % 2], dt[t][:, halves[h]], gs_t[:, t : t + 1], None, ALU.mult)
+        z4 = [new("z4_%d" % h, [P, HALF * PACK], BF16) for h in range(2)]
+        for h in range(2):
+            nc.vector.tensor_copy(
+                z4[h][:].bitcast(F32).rearrange("p (j u) -> p j u", u=2),
+                zp[h][:].rearrange("p u j e -> p u (j e)").bitcast(F32).rearrange("p u j -> p j u"),
+            )
         z_w = new("z_w", [P, S], U32)
         z_s = new("z_s", [P, S], U8)
-        nc.vector.quantize_mx(out=z_w[:].bitcast(FP8X4), scales=z_s[:], in_=z4[:])
-        hc_w = deal("hc_w_d", pick("hc_w", xw, hc_t, U32, tag="z4"), U32)
+        for h in range(2):
+            nc.vector.quantize_mx(out=z_w[:, halves[h]].bitcast(FP8X4), scales=z_s[:, halves[h]], in_=z4[h][:])
+        hc_w = deal("hc_w_d", pick("hc_w", xw, hc_t, U32, tag="z4_0"), U32)
 
-        def score(words, plane, t):
+        def score(words, plane, t, pieces):
             bank = psum.tile([P, S], F32, name="bank", tag="bank")
-            nc.tensor.matmul_mx(
-                out=bank[:],
-                lhsT=words[:, P * t : P * (t + 1)].bitcast(FP8X4),
-                lhsT_scale=plane[:, P * t : P * (t + 1)],
-                rhs=z_w[:].bitcast(FP8X4),
-                rhs_scale=z_s[:],
-                start=True,
-                stop=True,
-            )
+            for cols in pieces:
+                nc.tensor.matmul_mx(
+                    out=bank[:, cols],
+                    lhsT=words[:, P * t : P * (t + 1)].bitcast(FP8X4),
+                    lhsT_scale=plane[:, P * t : P * (t + 1)],
+                    rhs=z_w[:, cols].bitcast(FP8X4),
+                    rhs_scale=z_s[:, cols],
+                    start=True,
+                    stop=True,
+                )
             return bank
 
-        res = new("res", [P, PACK, S], F32)
+        whole = [slice(0, S)]
+        a_ps = [score(ca_w, ca_s, 0, halves), score(ca_w, ca_s, 1, whole)]
+        b_ps = [score(hc_w, hc_plane, 0, whole), score(hc_w, hc_plane, 1, whole)]
+        for t in range(2, PACK):
+            a_ps.append(score(ca_w, ca_s, t, whole))
+            b_ps.append(score(hc_w, hc_plane, t, whole))
+
+        def entries(offsets, cols):
+            return offsets[:, cols.start // 16 : cols.stop // 16]
+
+        def fetch(dst, bank):
+            nc.scalar.activation(dst[:, :S], bank[:], COPY, scale=SCORE_SCALE)
+
+        res = [new("res%d" % h, [P, PACK, HALF], F32) for h in range(2)]
         out_rows = out_0.rearrange("(p t) j -> p t j", t=PACK)
-        res4 = new("res4", [P, S * PACK], BF16)
-        res_w = new("res_w", [P, S], U32)
-        res_s = new("res_s", [P, S], U8)
-        out_words = out_1[0].rearrange("p n t -> p (n t)").bitcast(I32)
-        out_scales = out_2[0].bitcast(I32)
+        fetch(a_sb[0], a_ps[0])
+        nc.vector.tensor_scalar(a_sb[1][:, :S], a_ps[1][:], SCORE_SCALE, None, ALU.mult)
+        nc.vector.tensor_scalar(b_sb[0][:, :S], b_ps[0][:], SCORE_SCALE, None, ALU.mult)
         for t in range(PACK):
-            a_ps = score(ca_w, ca_s, t)
-            b_ps = score(hc_w, hc_plane, t)
-            nc.scalar.activation(a_sb[t][:, :S], a_ps[:], COPY, scale=SCORE_SCALE)
-            if t < 1:
-                nc.vector.tensor_scalar(b_sb[t][:, :S], b_ps[:], SCORE_SCALE, None, ALU.mult)
-            else:
-                nc.scalar.activation(b_sb[t][:, :S], b_ps[:], COPY, scale=SCORE_SCALE)
+            if t >= 2:
+                fetch(a_sb[t], a_ps[t])
+            if t >= 1:
+                fetch(b_sb[t], b_ps[t])
             a3 = new("a3_%d" % t, [P, S], F32)
             a4 = new("a4_%d" % t, [P, S], F32)
             s1 = new("s1_%d" % t, [P, S], F32)
             s2 = new("s2_%d" % t, [P, S], F32)
-            pieces = [(0, S)] if t < PACK - 1 else [(0, S // 2), (S // 2, S)]
-            for lo, hi in pieces:
-                cols = slice(lo // 16, hi // 16)
-                nc.scalar.activation(a3[:, lo:hi], a_sb[t][:].indirect(n3_t[:, cols]), COPY)
-                nc.scalar.activation(a4[:, lo:hi], a_sb[t][:].indirect(n4_t[:, cols]), COPY)
-                nc.vector.tensor_tensor(s1[:, lo:hi], b_sb[t][:].indirect(n5_t[:, cols]), a3[:, lo:hi], ALU.add)
-                nc.vector.tensor_tensor(s2[:, lo:hi], b_sb[t][:].indirect(n6_t[:, cols]), a4[:, lo:hi], ALU.add)
-                nc.vector.tensor_tensor(res[:, t, lo:hi], s1[:, lo:hi], s2[:, lo:hi], ALU.max)
-                nc.sync.dma_start(out_rows[:, t, lo:hi], res[:, t, lo:hi])
-                if t == PACK - 1:
-                    (nc.scalar.copy if lo == 0 else nc.vector.tensor_copy)(
-                        res4[:, PACK * lo : PACK * hi].rearrange("p (c i t) -> p c t i", i=4, t=PACK),
-                        res[:, :, lo:hi].rearrange("p t (c i) -> p c t i", i=4),
-                    )
-                    nc.vector.quantize_mx(
-                        out=res_w[:, lo:hi].bitcast(FP8X4), scales=res_s[:, lo:hi], in_=res4[:, PACK * lo : PACK * hi]
-                    )
-                    nc.sync.dma_start(out_words[:, lo:hi], res_w[:, lo:hi].bitcast(I32))
+
+
+            def look(dst, offsets, cols):
+                nc.scalar.activation(dst[:, cols], a_sb[t][:].indirect(entries(offsets, cols)), COPY)
+
+            def look_add(dst, offsets, other, cols):
+                nc.vector.tensor_tensor(dst[:, cols], b_sb[t][:].indirect(entries(offsets, cols)), other[:, cols], ALU.add)
+
+            def larger(h):
+                nc.vector.tensor_tensor(res[h][:, t, :], s1[:, halves[h]], s2[:, halves[h]], ALU.max)
+                nc.sync.dma_start(out_rows[:, t, halves[h]], res[h][:, t, :])
+
+            if t < PACK - 1:
+                look(a3, n3_t, whole[0])
+                look(a4, n4_t, whole[0])
+                look_add(s1, n5_t, a3, whole[0])
+                look_add(s2, n6_t, a4, halves[0])
+                look_add(s2, n6_t, a4, halves[1])
+                larger(0)
+                larger(1)
+            else:
+                for cols in halves:
+                    look(a3, n3_t, cols)
+                    look(a4, n4_t, cols)
+                look_add(s1, n5_t, a3, halves[0])
+                look_add(s2, n6_t, a4, halves[0])
+                look_add(s1, n5_t, a3, halves[1])
+                larger(0)
+                look_add(s2, n6_t, a4, halves[1])
+                larger(1)
+
+        res4 = [new("res4_%d" % h, [P, HALF * PACK], BF16) for h in range(2)]
+        res_w = new("res_w", [P, S], U32)
+        res_s = new("res_s", [P, S], U8)
+        out_words = out_1[0].rearrange("p n t -> p (n t)").bitcast(I32)
+        out_scales = out_2[0].bitcast(I32)
+        for h, copy in enumerate((nc.scalar.copy, nc.vector.tensor_copy)):
+            copy(
+                res4[h][:].rearrange("p (c i t) -> p c t i", i=4, t=PACK),
+                res[h][:].rearrange("p t (c i) -> p c t i", i=4),
+            )
+        for h in range(2):
+            nc.vector.quantize_mx(out=res_w[:, halves[h]].bitcast(FP8X4), scales=res_s[:, halves[h]], in_=res4[h][:])
+            nc.sync.dma_start(out_words[:, halves[h]], res_w[:, halves[h]].bitcast(I32))
         for q in range(4):
-            nc.scalar.dma_start(out_scales[4 * q : 4 * q + 4, :], res_s[32 * q : 32 * q + 4, :].bitcast(I32))
+            (nc.scalar, nc.sync)[q % 2].dma_start(out_scales[4 * q : 4 * q + 4, :], res_s[32 * q : 32 * q + 4, :].bitcast(I32))

@@ -95,28 +95,34 @@ def tile_picked_cdhpathborder_none_po_kernel(
             w1w_d[:].rearrange("p (t m b) -> p t m b", t=PACK, b=2), w1w[:].rearrange("p (m t b) -> p t m b", t=PACK, b=2)
         )
         xq_s = pick("xq_s", xs, offs_t, U8)
-        xq_w = pick("xq_w", xw, offs_t, U32)
-        w1s_d = deal("w1s_d", w1s, U8)
+        halves = [slice(0, HALF), slice(HALF, S)]
+        whole = [slice(0, S)]
 
-        y_ps = []
+        def entries(offsets, cols):
+            return offsets[:, cols.start // 16 : cols.stop // 16]
+
+        xq_w = new("xq_w", [P, S], U32)
+        nc.vector.tensor_copy(xq_w[:, halves[0]], xw[:].indirect(entries(offs_t, halves[0])))
+        w1s_d = new("w1s_d", [P, H], U8)
         for t in range(PACK):
-            bank = psum.tile([P, S], F32, name="bank", tag="bank")
+            nc.gpsimd.tensor_copy(w1s_d[:, P * t : P * (t + 1)], w1s[:, t:H:PACK])
+        nc.vector.tensor_copy(xq_w[:, halves[1]], xw[:].indirect(entries(offs_t, halves[1])))
+
+        y_ps = [psum.tile([P, S], F32, name="bank", tag="bank") for t in range(PACK)]
+        for t, cols in [(0, halves[0]), (1, halves[0]), (0, halves[1]), (1, halves[1]), (2, whole[0]), (3, whole[0])]:
             nc.tensor.matmul_mx(
-                out=bank[:],
+                out=y_ps[t][:, cols],
                 lhsT=w1w_d[:, 2 * P * t : 2 * P * (t + 1)].bitcast(FP4X4),
                 lhsT_scale=w1s_d[:, P * t : P * (t + 1)],
-                rhs=xq_w[:].bitcast(FP8X4),
-                rhs_scale=xq_s[:],
+                rhs=xq_w[:, cols].bitcast(FP8X4),
+                rhs_scale=xq_s[:, cols],
                 start=True,
                 stop=True,
             )
-            y_ps.append(bank)
 
         cand_s = new("cand_s", [P, 2, C], U8)
         nc.vector.tensor_copy(cand_s[:, 0, :], xs[:].indirect(ca_t[:]))
         nc.vector.tensor_copy(cand_s[:, 1, :], xs_runs[:].indirect(hc_t[:]))
-        ca_w = new("ca_w", [P, C], U32)
-        nc.vector.tensor_copy(ca_w[:].rearrange("p (t m) -> p m t", t=PACK), xw[:].indirect(ca_t[:]))
         cand_s_d = new("cand_s_d", [P, 2, C], U8)
         nc.vector.tensor_copy(
             cand_s_d[:].rearrange("p l (t m) -> p l t m", t=PACK), cand_s[:].rearrange("p l (m t) -> p l t m", t=PACK)
@@ -142,10 +148,11 @@ def tile_picked_cdhpathborder_none_po_kernel(
             nc.vector.tensor_tensor(ra[t][:], pa[t][:], pb[t][:], ALU.max)
             nc.vector.tensor_tensor(rb[t][:], pa[t][:], pb[t][:], ALU.min)
             nc.vector.tensor_copy(dt[t][:].indirect(n1_t[:]), ra[t][:])
+        ca_w = new("ca_w", [P, C], U32, tag="ra3")
+        nc.vector.tensor_copy(ca_w[:].rearrange("p (t m) -> p m t", t=PACK), xw[:].indirect(ca_t[:]))
         for t in range(PACK):
             nc.scalar.activation(dt[t][:].indirect(n2_t[:]), rb[t][:], COPY)
 
-        halves = [slice(0, HALF), slice(HALF, S)]
         zp = [new("zp%d" % h, [P, 2, HALF, 2], BF16) for h in range(2)]
         for t in range(PACK):
             for h in range(2):
@@ -176,15 +183,11 @@ def tile_picked_cdhpathborder_none_po_kernel(
                 )
             return bank
 
-        whole = [slice(0, S)]
         a_ps = [score(ca_w, ca_s, 0, halves), score(ca_w, ca_s, 1, whole)]
         b_ps = [score(hc_w, hc_plane, 0, whole), score(hc_w, hc_plane, 1, whole)]
         for t in range(2, PACK):
             a_ps.append(score(ca_w, ca_s, t, whole))
             b_ps.append(score(hc_w, hc_plane, t, whole))
-
-        def entries(offsets, cols):
-            return offsets[:, cols.start // 16 : cols.stop // 16]
 
         def fetch(dst, bank):
             nc.scalar.activation(dst[:, :S], bank[:], COPY, scale=SCORE_SCALE)

from contextlib import ExitStack

import concourse.mybir as mybir

K, T, S, H, W, C = 512, 2048, 512, 512, 256, 512
FLOPS = 2 * K * H * S + 2 * 2 * K * C * S

F32 = mybir.dt.float32
BF16 = mybir.dt.bfloat16
I32 = mybir.dt.int32
U32 = mybir.dt.uint32
U16 = mybir.dt.uint16
U8 = mybir.dt.uint8
FP8X4 = mybir.dt.float8_e4m3fn_x4
FP4X4 = mybir.dt.float4_e2m1fn_x4
ALU = mybir.AluOpType
COPY = mybir.ActivationFunctionType.Copy

P = 128
PACK = 4
SPARE = 16
SCORE_SCALE = 0.0625
HALF = S // 2


def tile_picked_cdhpathborder_none_po_kernel(
    tc, x_words, x_scales, w1_words, w1_scales, gs, offs, n1, n2, ca, hc, n3, n4, n5, n6, out_0, out_1, out_2
):
    nc = tc.nc
    with ExitStack() as ctx:
        lists = ctx.enter_context(tc.tile_pool(name="lists", bufs=1))
        sb = ctx.enter_context(tc.tile_pool(name="sb", bufs=1))
        psum = ctx.enter_context(tc.psum_pool(name="psum", bufs=8))

        def load_list(name, dram):
            tile = lists.tile(list(dram.shape), U16, name=name)
            nc.sync.dma_start(tile[:], dram)
            return tile

        def new(name, shape, dtype, tag=None):
            return sb.tile(shape, dtype, name=name, tag=tag or name, align_bytes=64)

        xs_rows = x_scales[0].bitcast(I32)
        w1s_rows = w1_scales[0].bitcast(I32)

        xs = new("xs", [P, T], U8)
        w1s = new("w1s", [P, H], U8)
        xs_runs = new("xs_runs", [P, T], U8)
        hc_plane = new("hc_plane", [P, C], U8)
        nc.gpsimd.memset(xs[:].bitcast(I32), 0)
        nc.vector.memset(w1s[:].bitcast(I32), 0)
        nc.gpsimd.memset(xs_runs[:].bitcast(I32), 0)
        nc.gpsimd.memset(hc_plane[:].bitcast(I32), 0)
        a_sb = [new("a%d" % t, [P, S + SPARE], F32) for t in range(PACK)]
        b_sb = [new("b%d" % t, [P, S + SPARE], F32) for t in range(PACK)]
        for tile in a_sb + b_sb:
            nc.gpsimd.memset(tile[:, S:], 0.0)

        offs_t = load_list("offs_t", offs)
        w1w = new("w1w", [P, 2 * H], U8)
        nc.sync.dma_start(w1w[:].bitcast(I32), w1_words[0].bitcast(I32))
        for q in range(4):
            nc.sync.dma_start(xs[32 * q : 32 * q + 4, :].bitcast(I32), xs_rows[4 * q : 4 * q + 4, :])
        xw = new("xw", [P, T], U32)
        nc.sync.dma_start(xw[:].bitcast(I32), x_words[0].rearrange("p n t -> p (n t)").bitcast(I32))
        for q in range(4):
            nc.sync.dma_start(w1s[32 * q : 32 * q + 4, :].bitcast(I32), w1s_rows[4 * q : 4 * q + 4, :])
        ca_t = load_list("ca_t", ca)
        n1_t = load_list("n1_t", n1)
        n2_t = load_list("n2_t", n2)
        hc_t = load_list("hc_t", hc)
        for e in range(2):
            nc.sync.dma_start(xs_runs[e:P:16, :].bitcast(I32), xs_rows[e:16:2, :])
        gs_t = new("gs_t", [P, PACK], F32)
        nc.sync.dma_start(gs_t[:], gs.rearrange("(p t) o -> p (t o)", t=PACK))
        n3_t = load_list("n3_t", n3)
        n4_t = load_list("n4_t", n4)
        n5_t = load_list("n5_t", n5)
        n6_t = load_list("n6_t", n6)

        def deal(name, src, dtype):
            dealt = new(name, [P, C], dtype)
            nc.vector.tensor_copy(
                dealt[:].rearrange("p (t m) -> p t m", t=PACK), src[:].rearrange("p (m t) -> p t m", t=PACK)
            )
            return dealt

        def pick(name, table, offsets, dtype, tag=None):
            picked = new(name, [P, C], dtype, tag)
            nc.vector.tensor_copy(picked[:], table[:].indirect(offsets[:]))
            return picked

        w1w_d = new("w1w_d", [P, 2 * H], U8)
        nc.vector.tensor_copy(
            w1w_d[:].rearrange("p (t m b) -> p t m b", t=PACK, b=2), w1w[:].rearrange("p (m t b) -> p t m b", t=PACK, b=2)
        )
        xq_s = pick("xq_s", xs, offs_t, U8)
        halves = [slice(0, HALF), slice(HALF, S)]
        whole = [slice(0, S)]

        def entries(offsets, cols):
            return offsets[:, cols.start // 16 : cols.stop // 16]

        xq_w = new("xq_w", [P, S], U32)
        nc.vector.tensor_copy(xq_w[:, halves[0]], xw[:].indirect(entries(offs_t, halves[0])))
        w1s_d = new("w1s_d", [P, H], U8)
        for t in range(PACK):
            nc.gpsimd.tensor_copy(w1s_d[:, P * t : P * (t + 1)], w1s[:, t:H:PACK])
        nc.vector.tensor_copy(xq_w[:, halves[1]], xw[:].indirect(entries(offs_t, halves[1])))

        y_ps = [psum.tile([P, S], F32, name="bank", tag="bank") for t in range(PACK)]
        for t, cols in [(0, halves[0]), (1, halves[0]), (0, halves[1]), (1, halves[1]), (2, whole[0]), (3, whole[0])]:
            nc.tensor.matmul_mx(
                out=y_ps[t][:, cols],
                lhsT=w1w_d[:, 2 * P * t : 2 * P * (t + 1)].bitcast(FP4X4),
                lhsT_scale=w1s_d[:, P * t : P * (t + 1)],
                rhs=xq_w[:, cols].bitcast(FP8X4),
                rhs_scale=xq_s[:, cols],
                start=True,
                stop=True,
            )

        cand_s = new("cand_s", [P, 2, C], U8)
        nc.vector.tensor_copy(cand_s[:, 0, :], xs[:].indirect(ca_t[:]))
        nc.vector.tensor_copy(cand_s[:, 1, :], xs_runs[:].indirect(hc_t[:]))
        cand_s_d = new("cand_s_d", [P, 2, C], U8)
        nc.vector.tensor_copy(
            cand_s_d[:].rearrange("p l (t m) -> p l t m", t=PACK), cand_s[:].rearrange("p l (m t) -> p l t m", t=PACK)
        )
        ca_s = cand_s_d[:, 0, :]
        for r in range(4):
            src = 16 * (r // 2) + r % 2
            nc.sync.dma_start(hc_plane[r:P:32, :].bitcast(I32), cand_s_d[src:P:32, 1, :].bitcast(I32))

        y = [new("y%d" % t, [P, S], F32) for t in range(PACK)]
        pa = [new("pa%d" % t, [P, W], F32) for t in range(PACK)]
        pb = [new("pb%d" % t, [P, W], F32) for t in range(PACK)]
        ra = [new("ra%d" % t, [P, W], F32) for t in range(PACK)]
        rb = [new("rb%d" % t, [P, W], F32) for t in range(PACK)]
        dt = [new("dt%d" % t, [P, S], F32) for t in range(PACK)]
        nc.scalar.copy(y[0][:], y_ps[0][:])
        for t in range(PACK):
            if t + 1 < PACK:
                nc.scalar.copy(y[t + 1][:], y_ps[t + 1][:])
            nc.scalar.activation(pa[t][:], y[t][:].indirect(n1_t[:]), COPY)
            nc.scalar.activation(pb[t][:], y[t][:].indirect(n2_t[:]), COPY)
        for t in range(PACK):
            nc.vector.tensor_tensor(ra[t][:], pa[t][:], pb[t][:], ALU.max)
            nc.vector.tensor_tensor(rb[t][:], pa[t][:], pb[t][:], ALU.min)
            nc.vector.tensor_copy(dt[t][:].indirect(n1_t[:]), ra[t][:])
        ca_w = new("ca_w", [P, C], U32, tag="ra3")
        nc.vector.tensor_copy(ca_w[:].rearrange("p (t m) -> p m t", t=PACK), xw[:].indirect(ca_t[:]))
        for t in range(PACK):
            nc.scalar.activation(dt[t][:].indirect(n2_t[:]), rb[t][:], COPY)

        zp = [new("zp%d" % h, [P, 2, HALF, 2], BF16) for h in range(2)]
        for t in range(PACK):
            for h in range(2):
                nc.vector.tensor_scalar(zp[h][:, t // 2, :, t % 2], dt[t][:, halves[h]], gs_t[:, t : t + 1], None, ALU.mult)
        z4 = [new("z4_%d" % h, [P, HALF * PACK], BF16) for h in range(2)]
        for h in range(2):
            nc.vector.tensor_copy(
                z4[h][:].bitcast(F32).rearrange("p (j u) -> p j u", u=2),
                zp[h][:].rearrange("p u j e -> p u (j e)").bitcast(F32).rearrange("p u j -> p j u"),
            )
        z_w = new("z_w", [P, S], U32)
        z_s = new("z_s", [P, S], U8)
        for h in range(2):
            nc.vector.quantize_mx(out=z_w[:, halves[h]].bitcast(FP8X4), scales=z_s[:, halves[h]], in_=z4[h][:])
        hc_w = deal("hc_w_d", pick("hc_w", xw, hc_t, U32, tag="z4_0"), U32)

        def score(words, plane, t, pieces):
            bank = psum.tile([P, S], F32, name="bank", tag="bank")
            for cols in pieces:
                nc.tensor.matmul_mx(
                    out=bank[:, cols],
                    lhsT=words[:, P * t : P * (t + 1)].bitcast(FP8X4),
                    lhsT_scale=plane[:, P * t : P * (t + 1)],
                    rhs=z_w[:, cols].bitcast(FP8X4),
                    rhs_scale=z_s[:, cols],
                    start=True,
                    stop=True,
                )
            return bank

        a_ps = [score(ca_w, ca_s, 0, halves), score(ca_w, ca_s, 1, whole)]
        b_ps = [score(hc_w, hc_plane, 0, whole), score(hc_w, hc_plane, 1, whole)]
        for t in range(2, PACK):
            a_ps.append(score(ca_w, ca_s, t, whole))
            b_ps.append(score(hc_w, hc_plane, t, whole))

        def fetch(dst, bank):
            nc.scalar.activation(dst[:, :S], bank[:], COPY, scale=SCORE_SCALE)

        res = [new("res%d" % h, [P, PACK, HALF], F32) for h in range(2)]
        out_rows = out_0.rearrange("(p t) j -> p t j", t=PACK)
        fetch(a_sb[0], a_ps[0])
        nc.vector.tensor_scalar(a_sb[1][:, :S], a_ps[1][:], SCORE_SCALE, None, ALU.mult)
        nc.vector.tensor_scalar(b_sb[0][:, :S], b_ps[0][:], SCORE_SCALE, None, ALU.mult)
        for t in range(PACK):
            if t >= 2:
                fetch(a_sb[t], a_ps[t])
            if t >= 1:
                fetch(b_sb[t], b_ps[t])
            a3 = new("a3_%d" % t, [P, S], F32)
            a4 = new("a4_%d" % t, [P, S], F32)
            s1 = new("s1_%d" % t, [P, S], F32)
            s2 = new("s2_%d" % t, [P, S], F32)


            def look(dst, offsets, cols):
                nc.scalar.activation(dst[:, cols], a_sb[t][:].indirect(entries(offsets, cols)), COPY)

            def look_add(dst, offsets, other, cols):
                nc.vector.tensor_tensor(dst[:, cols], b_sb[t][:].indirect(entries(offsets, cols)), other[:, cols], ALU.add)

            def larger(h):
                nc.vector.tensor_tensor(res[h][:, t, :], s1[:, halves[h]], s2[:, halves[h]], ALU.max)
                nc.sync.dma_start(out_rows[:, t, halves[h]], res[h][:, t, :])

            if t < PACK - 1:
                look(a3, n3_t, whole[0])
                look(a4, n4_t, whole[0])
                look_add(s1, n5_t, a3, whole[0])
                look_add(s2, n6_t, a4, halves[0])
                look_add(s2, n6_t, a4, halves[1])
                larger(0)
                larger(1)
            else:
                for cols in halves:
                    look(a3, n3_t, cols)
                    look(a4, n4_t, cols)
                look_add(s1, n5_t, a3, halves[0])
                look_add(s2, n6_t, a4, halves[0])
                look_add(s1, n5_t, a3, halves[1])
                larger(0)
                look_add(s2, n6_t, a4, halves[1])
                larger(1)

        res4 = [new("res4_%d" % h, [P, HALF * PACK], BF16) for h in range(2)]
        res_w = new("res_w", [P, S], U32)
        res_s = new("res_s", [P, S], U8)
        out_words = out_1[0].rearrange("p n t -> p (n t)").bitcast(I32)
        out_scales = out_2[0].bitcast(I32)
        for h, copy in enumerate((nc.scalar.copy, nc.vector.tensor_copy)):
            copy(
                res4[h][:].rearrange("p (c i t) -> p c t i", i=4, t=PACK),
                res[h][:].rearrange("p t (c i) -> p c t i", i=4),
            )
        for h in range(2):
            nc.vector.quantize_mx(out=res_w[:, halves[h]].bitcast(FP8X4), scales=res_s[:, halves[h]], in_=res4[h][:])
            nc.sync.dma_start(out_words[:, halves[h]], res_w[:, halves[h]].bitcast(I32))
        for q in range(4):
            (nc.scalar, nc.sync)[q % 2].dma_start(out_scales[4 * q : 4 * q + 4, :], res_s[32 * q : 32 * q + 4, :].bitcast(I32))
